import numpy as np
import ml_dtypes


def mxq(x, axis, fmt="e4m3"):
    dtype, down = {"e4m3": (ml_dtypes.float8_e4m3fn, 7), "e5m2": (ml_dtypes.float8_e5m2, 14)}[fmt]
    v = np.moveaxis(np.asarray(x, np.float32).astype(ml_dtypes.bfloat16).astype(np.float64), axis, -1)
    blocks = v.reshape(v.shape[:-1] + (-1, 32))
    amax = np.abs(blocks).max(-1, keepdims=True)
    byte = np.maximum(np.where(amax > 0, np.frexp(amax)[1] - 1 + 127, 0) - down, 1)
    scale = np.exp2(byte - 127.0)
    codes = (blocks / scale).astype(np.float32).astype(dtype).astype(np.float64)
    return np.moveaxis((codes * scale).reshape(v.shape), -1, axis)


WIDE = False


def mx_kscale(k):
    if not WIDE:
        return np.ones(k)
    levels = np.array([10, -10, 5, -5, 0])
    if k % 512:
        return np.exp2(np.random.permutation(np.resize(levels, k // 32))).repeat(32)
    a = np.empty((k // 512, 16))
    for p in range(k // 512):
        a[p, :8] = np.random.permutation(np.resize(levels, 8))
        for g in range(8):
            far = levels[np.abs(levels - a[p, g]) >= 10]
            a[p, g + 8] = far[np.random.randint(len(far))]
    return np.exp2(a.ravel()).repeat(32)


def f64(x):
    return np.asarray(x).astype(np.float64)


def striped(idx):
    return np.tile(idx.reshape(-1, 16).T, (8, 1)).astype(np.uint16)


def unstriped(offs):
    return offs[:16].T.reshape(-1).astype(np.int64)


def striped8(idx):
    return np.concatenate([x.reshape(-1, 16).T for x in idx]).astype(np.uint16)


def runs(offs, k):
    lists = np.stack([offs[16 * r : 16 * r + 16].T.reshape(-1) for r in range(8)]).astype(np.int64)
    return lists[np.arange(k) % 512 // 64]


def pack_weight(w):
    k, n = w.shape
    w = f64(np.asarray(w, np.float32).astype(ml_dtypes.bfloat16)).reshape(k // 32, 32, n)
    amax = np.abs(w).max(1)
    byte = np.clip(np.where(amax > 0, np.frexp(amax)[1] - 1 + 127 - 7, 1), 1, 254)
    scaled = (w * np.exp2(127.0 - byte)[:, None, :]).reshape(k, n).astype(np.float32)
    words = np.ascontiguousarray(scaled.reshape(k // 512, 128, 4, n).transpose(0, 1, 3, 2)).astype(ml_dtypes.float8_e4m3fn).view(np.uint8)
    return words, np.ascontiguousarray(byte.astype(np.uint8).reshape(k // 512, 16, n))


def unpack_weight(words, scales):
    g, p, n, _ = words.shape
    vals = np.ascontiguousarray(words).view(ml_dtypes.float8_e4m3fn).astype(np.float64) * np.repeat(np.exp2(scales.astype(np.float64) - 127.0), 8, axis=1)[..., None]
    return vals.transpose(0, 1, 3, 2).reshape(g * 512, n)


E2M1 = np.array([0.0, 0.5, 1.0, 1.5, 2.0, 3.0, 4.0, 6.0, -0.0, -0.5, -1.0, -1.5, -2.0, -3.0, -4.0, -6.0])


def pack_fp4(w):
    k, n = w.shape
    w = f64(np.asarray(w, np.float32).astype(ml_dtypes.bfloat16)).reshape(k // 32, 32, n)
    amax = np.abs(w).max(1)
    mant, ex = np.frexp(amax / 6.0)
    byte = np.clip(np.where(amax > 0, np.where(mant > 0.5, ex, ex - 1) + 127, 1), 1, 254)
    scaled = (w * np.exp2(127.0 - byte)[:, None, :]).reshape(k, n).astype(np.float32)
    c = np.ascontiguousarray(scaled.reshape(k // 512, 128, 4, n).transpose(0, 1, 3, 2)).astype(ml_dtypes.float4_e2m1fn).view(np.uint8) & 0xF
    words = (c[..., 0::2] | (c[..., 1::2] << 4)).reshape(k // 512, 128, 2 * n)
    return np.ascontiguousarray(words), np.ascontiguousarray(byte.astype(np.uint8).reshape(k // 512, 16, n))


def unpack_fp4(words, scales):
    g, _, n = scales.shape
    words = np.ascontiguousarray(words).reshape(g, 128, n, 2)
    nib = np.empty((g, 128, n, 4), np.uint8)
    nib[..., 0::2] = words & 0xF
    nib[..., 1::2] = words >> 4
    vals = E2M1[nib] * np.repeat(np.exp2(scales.astype(np.float64) - 127.0), 8, axis=1)[..., None]
    return vals.transpose(0, 1, 3, 2).reshape(g * 512, n)


def sigmoid(v):
    return 1.0 / (1.0 + np.exp(-np.maximum(v, -700.0)))


K, T, S, H, G = 512, 1024, 512, 512, 2048


def setup_inputs():
    n = np.random.standard_normal
    s = mx_kscale(K)[:, None]
    packed_xT = pack_weight(n((K, T)) * s)
    packed_w1 = pack_fp4(n((K, H)) / np.sqrt(2 * K) / s)
    packed_w2 = pack_fp4(n((K, H)) / np.sqrt(2 * K) / s)
    packed_dT = pack_weight(n((K, G)) / s)
    return {
        "x_words": packed_xT[0],
        "x_scales": packed_xT[1],
        "w1_words": packed_w1[0],
        "w1_scales": packed_w1[1],
        "w2_words": packed_w2[0],
        "w2_scales": packed_w2[1],
        "sl": np.random.uniform(1.0, 2.0, (H, 1)).astype(np.float32),
        "th": (0.5 * n((H, 1))).astype(np.float32),
        "gs": (np.random.uniform(0.5, 1.5, (K, 1)) * s).astype(np.float32),
        "d_words": packed_dT[0],
        "d_scales": packed_dT[1],
        "offs": striped(np.random.permutation(T)[:S]),
        "hz": striped8(np.random.randint(0, T, (8, S))),
        "n1": striped8(np.stack([np.random.permutation(S) for _ in range(8)])),
        "n2": striped8(np.stack([np.random.permutation(S) for _ in range(8)])),
        "ka": striped8(np.random.randint(0, G, (8, H))),
        "kb": striped8(np.random.randint(0, G, (8, H))),
        "n3": striped8(np.stack([np.random.permutation(S) for _ in range(8)])),
        "n4": striped8(np.stack([np.random.permutation(S) for _ in range(8)])),
    }


def reference(x_words, x_scales, w1_words, w1_scales, w2_words, w2_scales, sl, th, gs, d_words, d_scales, offs, hz, n1, n2, ka, kb, n3, n4):
    d_ka = unpack_weight(d_words, d_scales)[np.arange(K)[:, None], runs(ka, K)]
    xq = unpack_weight(x_words, x_scales)[:, unstriped(offs)]
    x_hz = unpack_weight(x_words, x_scales)[np.arange(K)[:, None], runs(hz, K)]
    y = unpack_fp4(w1_words, w1_scales).T @ xq + unpack_fp4(w2_words, w2_scales).T @ x_hz
    ds = np.zeros((H, S))
    ds[np.arange(H)[:, None], runs(n1, H)] = y
    sg = sigmoid(f64(sl) * (y[np.arange(H)[:, None], runs(n2, H)] - f64(th)))
    z = f64(gs) * (ds * sg)
    zq = mxq(z, 0, "e4m3")
    d_kb = unpack_weight(d_words, d_scales)[np.arange(K)[:, None], runs(kb, K)]
    h2 = 0.0625 * (d_ka.T @ zq + d_kb.T @ zq)
    ds2 = np.zeros((H, S))
    ds2[np.arange(H)[:, None], runs(n3, H)] = h2
    st = np.maximum(h2, ds2)
    ds3 = np.zeros((H, S))
    ds3[np.arange(H)[:, None], runs(n4, H)] = st
    return st - ds3

@@ -1,0 +1,272 @@
+from contextlib import ExitStack
+
+import concourse.mybir as mybir
+
+F32 = mybir.dt.float32
+BF16 = mybir.dt.bfloat16
+I32 = mybir.dt.int32
+U32 = mybir.dt.uint32
+U16 = mybir.dt.uint16
+U8 = mybir.dt.uint8
+FP8X4 = mybir.dt.float8_e4m3fn_x4
+FP4X4 = mybir.dt.float4_e2m1fn_x4
+ALU = mybir.AluOpType
+ACT = mybir.ActivationFunctionType
+
+P = 128
+PACK = 4
+T, S, H, G = 1024, 512, 512, 2048
+LIST_COLS = S // 16
+WIN = 2 * S
+FLOPS = 4 * 2 * 512 * 512 * 512
+
+
+def tile_picked_dthzaesndsndtwin_none_p_kernel(
+    tc, x_words, x_scales, w1_words, w1_scales, w2_words, w2_scales, sl, th, gs, d_words, d_scales,
+    offs, hz, n1, n2, ka, kb, n3, n4, out,
+):
+    nc = tc.nc
+    with ExitStack() as ctx:
+        lists = ctx.enter_context(tc.tile_pool(name="lists", bufs=1))
+        keep = ctx.enter_context(tc.tile_pool(name="keep", bufs=1))
+        psum = ctx.enter_context(tc.psum_pool(name="psum", bufs=1))
+
+        def load_list(src, name):
+            tile = lists.tile([P, LIST_COLS], U16, name=name)
+            nc.sync.dma_start(tile[:], src)
+            return tile
+
+        def zeroed_bytes(width, name, tag=""):
+            tile = keep.tile([P, width], U8, name=name, tag=tag, align_bytes=64)
+            nc.vector.memset(tile[:].bitcast(I32), 0)
+            return tile
+
+        def to_plane(plane, rows):
+            for r in range(4):
+                nc.sync.dma_start(plane[r:P:32, :].bitcast(I32), rows[8 * r:P:32, :].bitcast(I32))
+
+        x_bytes = zeroed_bytes(T, "x_bytes")
+        w_rows = zeroed_bytes(2 * H, "w_rows")
+        d_bytes = zeroed_bytes(G, "d_bytes", tag="ds0")
+        x_plane = zeroed_bytes(2 * S, "x_plane")
+        d_plane = zeroed_bytes(2 * H, "d_plane")
+
+        nc.scalar.dma_start(x_bytes[0:P:8, :].bitcast(I32), x_scales[0].bitcast(I32))
+        hz_l = load_list(hz, "hz_l")
+        offs_l = load_list(offs, "offs_l")
+        x_tab = keep.tile([P, T], I32, name="x_tab", align_bytes=64)
+        nc.sync.dma_start(x_tab[:], x_words[0].rearrange("p n t -> p (n t)").bitcast(I32))
+        for r in range(4):
+            nc.scalar.dma_start(w_rows[r:P:32, 0:H].bitcast(I32), w1_scales[0, r:16:4, :].bitcast(I32))
+        w_raw = []
+        for i, w_words in enumerate((w1_words, w2_words)):
+            raw = keep.tile([P, 2 * H], U8, name="w_raw%d" % i, align_bytes=64)
+            nc.sync.dma_start(raw[:].bitcast(I32), w_words[0].bitcast(I32))
+            w_raw.append(raw)
+        for r in range(4):
+            nc.scalar.dma_start(w_rows[r:P:32, H:2 * H].bitcast(I32), w2_scales[0, r:16:4, :].bitcast(I32))
+        nc.scalar.dma_start(d_bytes[0:P:8, :].bitcast(I32), d_scales[0].bitcast(I32))
+        ka_l = load_list(ka, "ka_l")
+
+        xg_bytes = keep.tile([P, 2 * S], U8, name="xg_bytes", align_bytes=64)
+        nc.vector.tensor_copy(xg_bytes[:, S:2 * S], x_bytes[:].indirect(hz_l[:]))
+        nc.vector.tensor_copy(xg_bytes[:, 0:S], x_bytes[:].indirect(offs_l[:]))
+        to_plane(x_plane, xg_bytes)
+
+        kb_l = load_list(kb, "kb_l")
+        n1_l = load_list(n1, "n1_l")
+        d_tab = keep.tile([P, G], I32, name="d_tab", align_bytes=64)
+        nc.sync.dma_start(d_tab[:], d_words[0].rearrange("p n t -> p (n t)").bitcast(I32))
+        n2_l = load_list(n2, "n2_l")
+        row_vals = []
+        for name, src in (("sl_t", sl), ("th_t", th), ("gs_t", gs)):
+            tile = keep.tile([P, PACK], F32, name=name)
+            nc.gpsimd.dma_start(tile[:], src.rearrange("(p t) o -> p (t o)", t=PACK))
+            row_vals.append(tile)
+        sl_t, th_t, gs_t = row_vals
+        n3_l = load_list(n3, "n3_l")
+        n4_l = load_list(n4, "n4_l")
+
+        xg_words = keep.tile([P, 2 * S], U32, name="xg_words", align_bytes=64)
+        nc.vector.tensor_copy(xg_words[:, 0:S], x_tab[:].bitcast(U32).indirect(offs_l[:]))
+
+        w_plane = keep.tile([P, 2 * H], U8, name="w_plane", align_bytes=64)
+        nc.vector.tensor_copy(
+            w_plane[:].rearrange("p (w t m) -> p w t m", w=2, t=PACK),
+            w_rows[:].rearrange("p (w m t) -> p w t m", w=2, t=PACK),
+        )
+        nc.vector.tensor_copy(xg_words[:, S:2 * S], x_tab[:].bitcast(U32).indirect(hz_l[:]))
+        w_codes = []
+        for i in range(2):
+            codes = keep.tile([P, 2 * H], U8, name="w_codes%d" % i, align_bytes=64)
+            nc.scalar.copy(
+                codes[:].bitcast(U16).rearrange("p (t m) -> p t m", t=PACK),
+                w_raw[i][:].bitcast(U16).rearrange("p (m t) -> p t m", t=PACK),
+            )
+            w_codes.append(codes)
+
+        dg_bytes = keep.tile([P, 2 * H], U8, name="dg_bytes", align_bytes=64)
+        nc.vector.tensor_copy(dg_bytes[:, 0:H], d_bytes[:].indirect(ka_l[:]))
+        nc.vector.tensor_copy(dg_bytes[:, H:2 * H], d_bytes[:].indirect(kb_l[:]))
+        neg_bias = keep.tile([P, PACK], F32, name="neg_bias")
+        nc.vector.scalar_tensor_tensor(neg_bias[:], sl_t[:], -1.0, th_t[:], ALU.mult, ALU.mult)
+        dd_bytes = keep.tile([P, 2 * H], U8, name="dd_bytes", align_bytes=64)
+
+        def deal_d_bytes(i):
+            nc.vector.tensor_copy(
+                dd_bytes[:, i * H:(i + 1) * H].rearrange("p (t m) -> p t m", t=PACK),
+                dg_bytes[:, i * H:(i + 1) * H].rearrange("p (m t) -> p t m", t=PACK),
+            )
+
+        deal_d_bytes(0)
+
+        y = []
+        for t in range(PACK):
+            acc = psum.tile([P, S], F32, name="y_acc%d" % t, tag="y_acc%d" % t)
+            for i in range(2):
+                nc.tensor.matmul_mx(
+                    out=acc[:],
+                    lhsT=w_codes[i][:, 2 * P * t:2 * P * (t + 1)].bitcast(FP4X4),
+                    lhsT_scale=w_plane[:, i * H + P * t:i * H + P * (t + 1)],
+                    rhs=xg_words[:, i * S:(i + 1) * S].bitcast(FP8X4),
+                    rhs_scale=x_plane[:, i * S:(i + 1) * S],
+                    start=(i == 0),
+                    stop=(i == 1),
+                )
+            y_t = keep.tile([P, S], F32, name="y%d" % t)
+            nc.scalar.copy(y_t[:], acc[:])
+            y.append(y_t)
+
+        z_rows = keep.tile([P, PACK, S], BF16, name="z_rows", align_bytes=64)
+        z_quads = keep.tile([P, S, PACK], BF16, name="z_quads", align_bytes=64)
+        ds, sg = [], []
+
+        def send_y(t):
+            ds_t = keep.tile([P, WIN], F32, name="ds%d" % t, tag="ds%d" % t, align_bytes=64)
+            nc.vector.tensor_copy(ds_t[:].indirect(n1_l[:]), y[t][:])
+            ds.append(ds_t)
+            sg_t = keep.tile([P, S], F32, name="sg%d" % t)
+            for half in range(2):
+                nc.scalar.activation(
+                    out=sg_t[:, half * S // 2:(half + 1) * S // 2],
+                    in_=y[t][:].indirect(n2_l[:, half * LIST_COLS // 2:(half + 1) * LIST_COLS // 2]),
+                    func=ACT.Sigmoid,
+                    scale=sl_t[:, t:t + 1],
+                    bias=neg_bias[:, t:t + 1],
+                )
+            sg.append(sg_t)
+
+        def make_z(t, cols=slice(0, S)):
+            nc.vector.scalar_tensor_tensor(
+                z_rows[:, t, cols], ds[t][:, cols], gs_t[:, t:t + 1], sg[t][:, cols], ALU.mult, ALU.mult
+            )
+
+        dg_words = keep.tile([P, 2 * H], U32, name="dg_words", align_bytes=64)
+        d_codes = keep.tile([P, 2 * H], U32, name="d_codes", align_bytes=64)
+
+        send_y(0)
+        deal_d_bytes(1)
+        to_plane(d_plane, dd_bytes)
+        send_y(1)
+        make_z(0)
+        send_y(2)
+        make_z(1)
+        nc.scalar.copy(z_quads[:, :, 0:2], z_rows[:, 0:2, :].rearrange("p t c -> p c t"))
+        send_y(3)
+        make_z(2)
+        halves = (slice(0, S // 2), slice(S // 2, S))
+        z_codes = keep.tile([P, S], U32, name="z_codes", align_bytes=64)
+        z_plane = keep.tile([P, S], U8, name="z_plane", align_bytes=64)
+
+        def weave(cols):
+            nc.vector.tensor_copy(z_quads[:, cols, 2:4], z_rows[:, 2:4, cols].rearrange("p t c -> p c t"))
+
+        def quantise(cols):
+            nc.vector.quantize_mx(
+                out=z_codes[:, cols].bitcast(FP8X4),
+                scales=z_plane[:, cols],
+                in_=z_quads[:, cols, :].rearrange("p c t -> p (c t)"),
+            )
+
+        nc.vector.tensor_copy(dg_words[:, 0:H], d_tab[:].bitcast(U32).indirect(ka_l[:]))
+        make_z(3, halves[0])
+        nc.vector.tensor_copy(dg_words[:, H:2 * H], d_tab[:].bitcast(U32).indirect(kb_l[:]))
+        weave(halves[0])
+        nc.vector.tensor_copy(
+            d_codes[:].rearrange("p (w t i m) -> p w i t m", w=2, t=PACK, m=4),
+            dg_words[:].rearrange("p (w i m t) -> p w i t m", w=2, t=PACK, m=4),
+        )
+        quantise(halves[0])
+        make_z(3, halves[1])
+        weave(halves[1])
+        quantise(halves[1])
+
+        h2 = [keep.tile([P, S], F32, name="h2_%d" % t) for t in range(PACK)]
+
+        def second_product(t, acc, cols):
+            for i in range(2):
+                nc.tensor.matmul_mx(
+                    out=acc,
+                    lhsT=d_codes[:, i * H + P * t:i * H + P * (t + 1)].bitcast(FP8X4),
+                    lhsT_scale=d_plane[:, i * H + P * t:i * H + P * (t + 1)],
+                    rhs=z_codes[:, cols].bitcast(FP8X4),
+                    rhs_scale=z_plane[:, cols],
+                    start=(i == 0),
+                    stop=(i == 1),
+                )
+            nc.scalar.activation(out=h2[t][:, cols], in_=acc, func=ACT.Copy, scale=0.0625)
+
+        for half, cols in enumerate(halves):
+            acc = psum.tile([P, S // 2], F32, name="h_half%d" % half, tag="y_acc%d" % half)
+            second_product(0, acc[:], cols)
+        h_acc = [None]
+        for t in range(1, PACK):
+            acc = psum.tile([P, S], F32, name="h_acc%d" % t)
+            second_product(t, acc[:], slice(0, S))
+            h_acc.append(acc)
+
+        ds2, st, ds3 = [], [], []
+        out_rows = out.rearrange("(p t) s -> p t s", t=PACK)
+
+        def send_h(t):
+            win = keep.tile([P, WIN], F32, name="ds2_%d" % t)
+            pieces = 2 if t == 0 else 1
+            for i in range(pieces):
+                lo, hi = i * LIST_COLS // pieces, (i + 1) * LIST_COLS // pieces
+                nc.vector.tensor_copy(win[:].indirect(n3_l[:, lo:hi]), h2[t][:, 16 * lo:16 * hi])
+            ds2.append(win)
+
+        def larger(t):
+            st_t = keep.tile([P, S], F32, name="st%d" % t)
+            if t == 0:
+                nc.vector.tensor_tensor(st_t[:], h2[t][:], ds2[t][:, 0:S], ALU.max)
+            else:
+                nc.vector.scalar_tensor_tensor(st_t[:], h_acc[t][:], 0.0625, ds2[t][:, 0:S], ALU.mult, ALU.max)
+            st.append(st_t)
+
+        def send_st(t):
+            win = keep.tile([P, WIN], F32, name="ds3_%d" % t)
+            nc.vector.tensor_copy(win[:].indirect(n4_l[:]), st[t][:])
+            ds3.append(win)
+
+        def finish(t):
+            res = keep.tile([P, S], F32, name="res%d" % t)
+            nc.vector.tensor_tensor(res[:], st[t][:], ds3[t][:, 0:S], ALU.subtract)
+            nc.sync.dma_start(out_rows[:, t, :], res[:])
+
+        send_h(0)
+        send_h(1)
+        larger(0)
+        send_h(2)
+        larger(1)
+        send_h(3)
+        larger(2)
+        send_st(0)
+        larger(3)
+        send_st(1)
+        finish(0)
+        send_st(2)
+        finish(1)
+        send_st(3)
+        finish(2)
+        finish(3)

@@ -41,61 +41,55 @@ def tile_picked_dthzaesndsndtwin_none_p_kernel(
             nc.vector.memset(tile[:].bitcast(I32), 0)
             return tile
 
-        def to_plane(plane, rows):
+        def to_plane(queue, plane, rows):
             for r in range(4):
-                nc.sync.dma_start(plane[r:P:32, :].bitcast(I32), rows[8 * r:P:32, :].bitcast(I32))
+                queue.dma_start(plane[r:P:32, :].bitcast(I32), rows[8 * r:P:32, :].bitcast(I32))
 
-        x_bytes = zeroed_bytes(T, "x_bytes")
-        w_rows = zeroed_bytes(2 * H, "w_rows")
+        x_bytes = zeroed_bytes(T, "x_bytes", tag="d_tab")
+        w_rows = zeroed_bytes(2 * H, "w_rows", tag="w_rows")
         d_bytes = zeroed_bytes(G, "d_bytes", tag="ds0")
         x_plane = zeroed_bytes(2 * S, "x_plane")
         d_plane = zeroed_bytes(2 * H, "d_plane")
 
+        def load_words(src, name):
+            raw = keep.tile([P, 2 * H], U8, name=name, tag=name, align_bytes=64)
+            nc.sync.dma_start(raw[:].bitcast(I32), src[0].bitcast(I32))
+            return raw
+
         nc.scalar.dma_start(x_bytes[0:P:8, :].bitcast(I32), x_scales[0].bitcast(I32))
         hz_l = load_list(hz, "hz_l")
         offs_l = load_list(offs, "offs_l")
-        x_tab = keep.tile([P, T], I32, name="x_tab", align_bytes=64)
+        x_tab = keep.tile([P, T], I32, name="x_tab", tag="x_tab", align_bytes=64)
         nc.sync.dma_start(x_tab[:], x_words[0].rearrange("p n t -> p (n t)").bitcast(I32))
-        for r in range(4):
-            nc.scalar.dma_start(w_rows[r:P:32, 0:H].bitcast(I32), w1_scales[0, r:16:4, :].bitcast(I32))
-        w_raw = []
-        for i, w_words in enumerate((w1_words, w2_words)):
-            raw = keep.tile([P, 2 * H], U8, name="w_raw%d" % i, align_bytes=64)
-            nc.sync.dma_start(raw[:].bitcast(I32), w_words[0].bitcast(I32))
-            w_raw.append(raw)
-        for r in range(4):
-            nc.scalar.dma_start(w_rows[r:P:32, H:2 * H].bitcast(I32), w2_scales[0, r:16:4, :].bitcast(I32))
-        nc.scalar.dma_start(d_bytes[0:P:8, :].bitcast(I32), d_scales[0].bitcast(I32))
         ka_l = load_list(ka, "ka_l")
+        kb_l = load_list(kb, "kb_l")
+        w_raw = [load_words(w1_words, "w_raw0")]
+        n1_l = load_list(n1, "n1_l")
+        w_raw.append(load_words(w2_words, "w_raw1"))
+        for i, w_scales in enumerate((w1_scales, w2_scales)):
+            for r in range(4):
+                nc.scalar.dma_start(w_rows[r:P:32, i * H:(i + 1) * H].bitcast(I32), w_scales[0, r:16:4, :].bitcast(I32))
+        nc.gpsimd.dma_start(d_bytes[0:P:8, :].bitcast(I32), d_scales[0].bitcast(I32))
 
         xg_bytes = keep.tile([P, 2 * S], U8, name="xg_bytes", align_bytes=64)
         nc.vector.tensor_copy(xg_bytes[:, S:2 * S], x_bytes[:].indirect(hz_l[:]))
         nc.vector.tensor_copy(xg_bytes[:, 0:S], x_bytes[:].indirect(offs_l[:]))
-        to_plane(x_plane, xg_bytes)
+        to_plane(nc.sync, x_plane, xg_bytes)
 
-        kb_l = load_list(kb, "kb_l")
-        n1_l = load_list(n1, "n1_l")
-        d_tab = keep.tile([P, G], I32, name="d_tab", align_bytes=64)
-        nc.sync.dma_start(d_tab[:], d_words[0].rearrange("p n t -> p (n t)").bitcast(I32))
         n2_l = load_list(n2, "n2_l")
-        row_vals = []
-        for name, src in (("sl_t", sl), ("th_t", th), ("gs_t", gs)):
-            tile = keep.tile([P, PACK], F32, name=name)
-            nc.gpsimd.dma_start(tile[:], src.rearrange("(p t) o -> p (t o)", t=PACK))
-            row_vals.append(tile)
-        sl_t, th_t, gs_t = row_vals
         n3_l = load_list(n3, "n3_l")
         n4_l = load_list(n4, "n4_l")
-
+        d_tab = keep.tile([P, G], I32, name="d_tab", tag="d_tab", align_bytes=64)
+        nc.sync.dma_start(d_tab[:], d_words[0].rearrange("p n t -> p (n t)").bitcast(I32))
         xg_words = keep.tile([P, 2 * S], U32, name="xg_words", align_bytes=64)
         nc.vector.tensor_copy(xg_words[:, 0:S], x_tab[:].bitcast(U32).indirect(offs_l[:]))
+        nc.vector.tensor_copy(xg_words[:, S:2 * S], x_tab[:].bitcast(U32).indirect(hz_l[:]))
 
         w_plane = keep.tile([P, 2 * H], U8, name="w_plane", align_bytes=64)
         nc.vector.tensor_copy(
             w_plane[:].rearrange("p (w t m) -> p w t m", w=2, t=PACK),
             w_rows[:].rearrange("p (w m t) -> p w t m", w=2, t=PACK),
         )
-        nc.vector.tensor_copy(xg_words[:, S:2 * S], x_tab[:].bitcast(U32).indirect(hz_l[:]))
         w_codes = []
         for i in range(2):
             codes = keep.tile([P, 2 * H], U8, name="w_codes%d" % i, align_bytes=64)
@@ -105,11 +99,20 @@ def tile_picked_dthzaesndsndtwin_none_p_kernel(
             )
             w_codes.append(codes)
 
-        dg_bytes = keep.tile([P, 2 * H], U8, name="dg_bytes", align_bytes=64)
+        row_vals = []
+        for name, src, tag in (("sl_t", sl, "w_raw0"), ("th_t", th, "w_raw1"), ("gs_t", gs, "x_tab")):
+            tile = keep.tile([P, PACK], F32, name=name, tag=tag, align_bytes=64)
+            nc.gpsimd.dma_start(tile[:], src.rearrange("(p t) o -> p (t o)", t=PACK))
+            row_vals.append(tile)
+        sl_t, th_t, gs_t = row_vals
+
+        dg_bytes = keep.tile([P, 2 * H], U8, name="dg_bytes", tag="w_rows", align_bytes=64)
         nc.vector.tensor_copy(dg_bytes[:, 0:H], d_bytes[:].indirect(ka_l[:]))
         nc.vector.tensor_copy(dg_bytes[:, H:2 * H], d_bytes[:].indirect(kb_l[:]))
-        neg_bias = keep.tile([P, PACK], F32, name="neg_bias")
-        nc.vector.scalar_tensor_tensor(neg_bias[:], sl_t[:], -1.0, th_t[:], ALU.mult, ALU.mult)
+        sl_th = keep.tile([P, PACK], F32, name="sl_th")
+        nc.gpsimd.tensor_tensor(sl_th[:], sl_t[:], th_t[:], ALU.mult)
+        neg_bias = keep.tile([P, PACK], F32, name="neg_bias", tag="z_quads", align_bytes=64)
+        nc.gpsimd.tensor_scalar(neg_bias[:], sl_th[:], -1.0, 0.0, ALU.mult, ALU.add)
         dd_bytes = keep.tile([P, 2 * H], U8, name="dd_bytes", align_bytes=64)
 
         def deal_d_bytes(i):
@@ -133,12 +136,12 @@ def tile_picked_dthzaesndsndtwin_none_p_kernel(
                     start=(i == 0),
                     stop=(i == 1),
                 )
-            y_t = keep.tile([P, S], F32, name="y%d" % t)
+            y_t = keep.tile([P, S], F32, name="y%d" % t, tag="y%d" % t, align_bytes=64)
             nc.scalar.copy(y_t[:], acc[:])
             y.append(y_t)
 
         z_rows = keep.tile([P, PACK, S], BF16, name="z_rows", align_bytes=64)
-        z_quads = keep.tile([P, S, PACK], BF16, name="z_quads", align_bytes=64)
+        z_quads = keep.tile([P, S, PACK], BF16, name="z_quads", tag="z_quads", align_bytes=64)
         ds, sg = [], []
 
         def send_y(t):
@@ -161,19 +164,24 @@ def tile_picked_dthzaesndsndtwin_none_p_kernel(
                 z_rows[:, t, cols], ds[t][:, cols], gs_t[:, t:t + 1], sg[t][:, cols], ALU.mult, ALU.mult
             )
 
-        dg_words = keep.tile([P, 2 * H], U32, name="dg_words", align_bytes=64)
+        def make_z_aside(t):
+            gated = keep.tile([P, S], F32, name="gated%d" % t)
+            nc.gpsimd.tensor_tensor(gated[:], ds[t][:, 0:S], sg[t][:], ALU.mult)
+            target = z_quads[:, :, t] if t < 2 else z_rows[:, t, :]
+            nc.scalar.activation(out=target, in_=gated[:], func=ACT.Copy, scale=gs_t[:, t:t + 1])
+
+        dg_words = keep.tile([P, 2 * H], U32, name="dg_words", tag="y2", align_bytes=64)
         d_codes = keep.tile([P, 2 * H], U32, name="d_codes", align_bytes=64)
 
         send_y(0)
         deal_d_bytes(1)
-        to_plane(d_plane, dd_bytes)
+        to_plane(nc.sync, d_plane, dd_bytes)
         send_y(1)
-        make_z(0)
+        make_z_aside(0)
         send_y(2)
-        make_z(1)
-        nc.scalar.copy(z_quads[:, :, 0:2], z_rows[:, 0:2, :].rearrange("p t c -> p c t"))
+        make_z_aside(1)
         send_y(3)
-        make_z(2)
+        make_z_aside(2)
         halves = (slice(0, S // 2), slice(S // 2, S))
         z_codes = keep.tile([P, S], U32, name="z_codes", align_bytes=64)
         z_plane = keep.tile([P, S], U8, name="z_plane", align_bytes=64)
@@ -251,7 +259,8 @@ def tile_picked_dthzaesndsndtwin_none_p_kernel(
 
         def finish(t):
             res = keep.tile([P, S], F32, name="res%d" % t)
-            nc.vector.tensor_tensor(res[:], st[t][:], ds3[t][:, 0:S], ALU.subtract)
+            engine = nc.vector if t == PACK - 1 else nc.gpsimd
+            engine.tensor_tensor(res[:], st[t][:], ds3[t][:, 0:S], ALU.subtract)
             nc.sync.dma_start(out_rows[:, t, :], res[:])
 
         send_h(0)

@@ -56,19 +56,25 @@ def tile_picked_dthzaesndsndtwin_none_p_kernel(
             nc.sync.dma_start(raw[:].bitcast(I32), src[0].bitcast(I32))
             return raw
 
+        def load_w_rows(queue, i, r):
+            w_scales = (w1_scales, w2_scales)[i]
+            queue.dma_start(w_rows[r:P:32, i * H:(i + 1) * H].bitcast(I32), w_scales[0, r:16:4, :].bitcast(I32))
+
         nc.scalar.dma_start(x_bytes[0:P:8, :].bitcast(I32), x_scales[0].bitcast(I32))
         hz_l = load_list(hz, "hz_l")
         offs_l = load_list(offs, "offs_l")
-        x_tab = keep.tile([P, T], I32, name="x_tab", tag="x_tab", align_bytes=64)
-        nc.sync.dma_start(x_tab[:], x_words[0].rearrange("p n t -> p (n t)").bitcast(I32))
         ka_l = load_list(ka, "ka_l")
         kb_l = load_list(kb, "kb_l")
+        load_w_rows(nc.sync, 0, 0)
+        x_tab = keep.tile([P, T], I32, name="x_tab", tag="x_tab", align_bytes=64)
+        nc.sync.dma_start(x_tab[:], x_words[0].rearrange("p n t -> p (n t)").bitcast(I32))
         w_raw = [load_words(w1_words, "w_raw0")]
+        for i, r in ((0, 1), (0, 2), (0, 3), (1, 0), (1, 1)):
+            load_w_rows(nc.sync, i, r)
         n1_l = load_list(n1, "n1_l")
         w_raw.append(load_words(w2_words, "w_raw1"))
-        for i, w_scales in enumerate((w1_scales, w2_scales)):
-            for r in range(4):
-                nc.scalar.dma_start(w_rows[r:P:32, i * H:(i + 1) * H].bitcast(I32), w_scales[0, r:16:4, :].bitcast(I32))
+        for r in (2, 3):
+            load_w_rows(nc.gpsimd, 1, r)
         nc.gpsimd.dma_start(d_bytes[0:P:8, :].bitcast(I32), d_scales[0].bitcast(I32))
 
         xg_bytes = keep.tile([P, 2 * S], U8, name="xg_bytes", align_bytes=64)
@@ -125,7 +131,7 @@ def tile_picked_dthzaesndsndtwin_none_p_kernel(
 
         y = []
         for t in range(PACK):
-            acc = psum.tile([P, S], F32, name="y_acc%d" % t, tag="y_acc%d" % t)
+            acc = psum.tile([P, S], F32, name="y_acc%d" % t, tag="bank%d" % t)
             for i in range(2):
                 nc.tensor.matmul_mx(
                     out=acc[:],
@@ -140,7 +146,6 @@ def tile_picked_dthzaesndsndtwin_none_p_kernel(
             nc.scalar.copy(y_t[:], acc[:])
             y.append(y_t)
 
-        z_rows = keep.tile([P, PACK, S], BF16, name="z_rows", align_bytes=64)
         z_quads = keep.tile([P, S, PACK], BF16, name="z_quads", tag="z_quads", align_bytes=64)
         ds, sg = [], []
 
@@ -160,34 +165,25 @@ def tile_picked_dthzaesndsndtwin_none_p_kernel(
             sg.append(sg_t)
 
         def make_z(t, cols=slice(0, S)):
-            nc.vector.scalar_tensor_tensor(
-                z_rows[:, t, cols], ds[t][:, cols], gs_t[:, t:t + 1], sg[t][:, cols], ALU.mult, ALU.mult
-            )
-
-        def make_z_aside(t):
-            gated = keep.tile([P, S], F32, name="gated%d" % t)
-            nc.gpsimd.tensor_tensor(gated[:], ds[t][:, 0:S], sg[t][:], ALU.mult)
-            target = z_quads[:, :, t] if t < 2 else z_rows[:, t, :]
-            nc.scalar.activation(out=target, in_=gated[:], func=ACT.Copy, scale=gs_t[:, t:t + 1])
+            gated = keep.tile([P, cols.stop - cols.start], F32, name="gated%d_%d" % (t, cols.start))
+            nc.gpsimd.tensor_tensor(gated[:], ds[t][:, cols], sg[t][:, cols], ALU.mult)
+            nc.scalar.activation(out=z_quads[:, cols, t], in_=gated[:], func=ACT.Copy, scale=gs_t[:, t:t + 1])
 
         dg_words = keep.tile([P, 2 * H], U32, name="dg_words", tag="y2", align_bytes=64)
-        d_codes = keep.tile([P, 2 * H], U32, name="d_codes", align_bytes=64)
+        d_codes = [keep.tile([P, 2, 2, P], U32, name="d_codes%d" % u, align_bytes=64) for u in range(2)]
 
         send_y(0)
         deal_d_bytes(1)
         to_plane(nc.sync, d_plane, dd_bytes)
         send_y(1)
-        make_z_aside(0)
+        make_z(0)
         send_y(2)
-        make_z_aside(1)
+        make_z(1)
         send_y(3)
-        make_z_aside(2)
-        halves = (slice(0, S // 2), slice(S // 2, S))
+        make_z(2)
+        head, middle, last, rest = slice(0, 128), slice(128, 384), slice(384, S), slice(128, S)
         z_codes = keep.tile([P, S], U32, name="z_codes", align_bytes=64)
         z_plane = keep.tile([P, S], U8, name="z_plane", align_bytes=64)
-
-        def weave(cols):
-            nc.vector.tensor_copy(z_quads[:, cols, 2:4], z_rows[:, 2:4, cols].rearrange("p t c -> p c t"))
 
         def quantise(cols):
             nc.vector.quantize_mx(
@@ -196,60 +192,63 @@ def tile_picked_dthzaesndsndtwin_none_p_kernel(
                 in_=z_quads[:, cols, :].rearrange("p c t -> p (c t)"),
             )
 
+        def deal_d_words(u):
+            nc.vector.tensor_copy(
+                d_codes[u][:].rearrange("p w t (i m) -> p w i t m", m=4),
+                dg_words[:].rearrange("p (w i m t) -> p w i t m", w=2, t=PACK, m=4)[:, :, :, 2 * u:2 * u + 2, :],
+            )
+
+        for cols in (slice(0, S // 2), slice(S // 2, S)):
+            make_z(3, cols)
         nc.vector.tensor_copy(dg_words[:, 0:H], d_tab[:].bitcast(U32).indirect(ka_l[:]))
-        make_z(3, halves[0])
         nc.vector.tensor_copy(dg_words[:, H:2 * H], d_tab[:].bitcast(U32).indirect(kb_l[:]))
-        weave(halves[0])
-        nc.vector.tensor_copy(
-            d_codes[:].rearrange("p (w t i m) -> p w i t m", w=2, t=PACK, m=4),
-            dg_words[:].rearrange("p (w i m t) -> p w i t m", w=2, t=PACK, m=4),
-        )
-        quantise(halves[0])
-        make_z(3, halves[1])
-        weave(halves[1])
-        quantise(halves[1])
+        quantise(head)
+        deal_d_words(0)
+        quantise(rest)
+        deal_d_words(1)
 
-        h2 = [keep.tile([P, S], F32, name="h2_%d" % t) for t in range(PACK)]
+        h2 = [keep.tile([P, 2, S], F32, name="h2_%d" % u) for u in range(2)]
 
-        def second_product(t, acc, cols):
-            for i in range(2):
-                nc.tensor.matmul_mx(
-                    out=acc,
-                    lhsT=d_codes[:, i * H + P * t:i * H + P * (t + 1)].bitcast(FP8X4),
-                    lhsT_scale=d_plane[:, i * H + P * t:i * H + P * (t + 1)],
-                    rhs=z_codes[:, cols].bitcast(FP8X4),
-                    rhs_scale=z_plane[:, cols],
-                    start=(i == 0),
-                    stop=(i == 1),
-                )
-            nc.scalar.activation(out=h2[t][:, cols], in_=acc, func=ACT.Copy, scale=0.0625)
+        def second_product(bank, tiles, cols):
+            width = cols.stop - cols.start
+            acc = psum.tile([P, len(tiles), width], F32, name="h_acc%d" % bank, tag="bank%d" % bank)
+            for j, t in enumerate(tiles):
+                for i in range(2):
+                    nc.tensor.matmul_mx(
+                        out=acc[:, j, :],
+                        lhsT=d_codes[t // 2][:, i, t % 2, :].bitcast(FP8X4),
+                        lhsT_scale=d_plane[:, i * H + P * t:i * H + P * (t + 1)],
+                        rhs=z_codes[:, cols].bitcast(FP8X4),
+                        rhs_scale=z_plane[:, cols],
+                        start=(i == 0),
+                        stop=(i == 1),
+                    )
+            first = tiles[0]
+            nc.scalar.activation(
+                out=h2[first // 2][:, first % 2:first % 2 + len(tiles), cols], in_=acc[:], func=ACT.Copy, scale=0.0625
+            )
 
-        for half, cols in enumerate(halves):
-            acc = psum.tile([P, S // 2], F32, name="h_half%d" % half, tag="y_acc%d" % half)
-            second_product(0, acc[:], cols)
-        h_acc = [None]
-        for t in range(1, PACK):
-            acc = psum.tile([P, S], F32, name="h_acc%d" % t)
-            second_product(t, acc[:], slice(0, S))
-            h_acc.append(acc)
+        second_product(0, (0,), head)
+        second_product(1, (1,), head)
+        second_product(2, (0, 1), middle)
+        second_product(3, (0, 1), last)
+        second_product(4, (2, 3), slice(0, S // 2))
+        second_product(5, (2, 3), slice(S // 2, S))
 
         ds2, st, ds3 = [], [], []
         out_rows = out.rearrange("(p t) s -> p t s", t=PACK)
 
-        def send_h(t):
-            win = keep.tile([P, WIN], F32, name="ds2_%d" % t)
-            pieces = 2 if t == 0 else 1
-            for i in range(pieces):
-                lo, hi = i * LIST_COLS // pieces, (i + 1) * LIST_COLS // pieces
-                nc.vector.tensor_copy(win[:].indirect(n3_l[:, lo:hi]), h2[t][:, 16 * lo:16 * hi])
-            ds2.append(win)
+        for t in range(PACK):
+            ds2.append(keep.tile([P, WIN], F32, name="ds2_%d" % t))
+
+        def send_h(t, cols):
+            nc.vector.tensor_copy(
+                ds2[t][:].indirect(n3_l[:, cols.start // 16:cols.stop // 16]), h2[t // 2][:, t % 2, cols]
+            )
 
         def larger(t):
             st_t = keep.tile([P, S], F32, name="st%d" % t)
-            if t == 0:
-                nc.vector.tensor_tensor(st_t[:], h2[t][:], ds2[t][:, 0:S], ALU.max)
-            else:
-                nc.vector.scalar_tensor_tensor(st_t[:], h_acc[t][:], 0.0625, ds2[t][:, 0:S], ALU.mult, ALU.max)
+            nc.vector.tensor_tensor(st_t[:], h2[t // 2][:, t % 2, :], ds2[t][:, 0:S], ALU.max)
             st.append(st_t)
 
         def send_st(t):
@@ -259,23 +258,25 @@ def tile_picked_dthzaesndsndtwin_none_p_kernel(
 
         def finish(t):
             res = keep.tile([P, S], F32, name="res%d" % t)
-            engine = nc.vector if t == PACK - 1 else nc.gpsimd
-            engine.tensor_tensor(res[:], st[t][:], ds3[t][:, 0:S], ALU.subtract)
-            nc.sync.dma_start(out_rows[:, t, :], res[:])
+            if t < PACK - 1:
+                nc.gpsimd.tensor_tensor(res[:], st[t][:], ds3[t][:, 0:S], ALU.subtract)
+                nc.sync.dma_start(out_rows[:, t, :], res[:])
+            else:
+                for queue, cols in ((nc.sync, slice(0, S // 2)), (nc.scalar, slice(S // 2, S))):
+                    nc.vector.tensor_tensor(res[:, cols], st[t][:, cols], ds3[t][:, cols], ALU.subtract)
+                    queue.dma_start(out_rows[:, t, cols], res[:, cols])
 
-        send_h(0)
-        send_h(1)
+        for cols in (head, rest):
+            send_h(0, cols)
+            send_h(1, cols)
         larger(0)
-        send_h(2)
+        send_h(2, slice(0, S))
         larger(1)
-        send_h(3)
+        send_h(3, slice(0, S))
         larger(2)
-        send_st(0)
         larger(3)
-        send_st(1)
-        finish(0)
-        send_st(2)
-        finish(1)
-        send_st(3)
-        finish(2)
-        finish(3)
+        send_st(0)
+        for t in range(1, PACK):
+            send_st(t)
+            finish(t - 1)
+        finish(PACK - 1)

@@ -45,7 +45,7 @@ def tile_picked_dthzaesndsndtwin_none_p_kernel(
             for r in range(4):
                 queue.dma_start(plane[r:P:32, :].bitcast(I32), rows[8 * r:P:32, :].bitcast(I32))
 
-        x_bytes = zeroed_bytes(T, "x_bytes", tag="d_tab")
+        x_bytes = zeroed_bytes(T, "x_bytes", tag="x_bytes")
         w_rows = zeroed_bytes(2 * H, "w_rows", tag="w_rows")
         d_bytes = zeroed_bytes(G, "d_bytes", tag="ds0")
         x_plane = zeroed_bytes(2 * S, "x_plane")
@@ -85,11 +85,11 @@ def tile_picked_dthzaesndsndtwin_none_p_kernel(
         n2_l = load_list(n2, "n2_l")
         n3_l = load_list(n3, "n3_l")
         n4_l = load_list(n4, "n4_l")
-        d_tab = keep.tile([P, G], I32, name="d_tab", tag="d_tab", align_bytes=64)
-        nc.sync.dma_start(d_tab[:], d_words[0].rearrange("p n t -> p (n t)").bitcast(I32))
         xg_words = keep.tile([P, 2 * S], U32, name="xg_words", align_bytes=64)
         nc.vector.tensor_copy(xg_words[:, 0:S], x_tab[:].bitcast(U32).indirect(offs_l[:]))
         nc.vector.tensor_copy(xg_words[:, S:2 * S], x_tab[:].bitcast(U32).indirect(hz_l[:]))
+        d_tab = keep.tile([P, G], I32, name="d_tab", tag="x_tab", align_bytes=64)
+        nc.sync.dma_start(d_tab[:], d_words[0].rearrange("p n t -> p (n t)").bitcast(I32))
 
         w_plane = keep.tile([P, 2 * H], U8, name="w_plane", align_bytes=64)
         nc.vector.tensor_copy(
@@ -106,7 +106,7 @@ def tile_picked_dthzaesndsndtwin_none_p_kernel(
             w_codes.append(codes)
 
         row_vals = []
-        for name, src, tag in (("sl_t", sl, "w_raw0"), ("th_t", th, "w_raw1"), ("gs_t", gs, "x_tab")):
+        for name, src, tag in (("sl_t", sl, "w_raw0"), ("th_t", th, "w_raw1"), ("gs_t", gs, "x_bytes")):
             tile = keep.tile([P, PACK], F32, name=name, tag=tag, align_bytes=64)
             nc.gpsimd.dma_start(tile[:], src.rearrange("(p t) o -> p (t o)", t=PACK))
             row_vals.append(tile)

from contextlib import ExitStack

import concourse.mybir as mybir

F32 = mybir.dt.float32
BF16 = mybir.dt.bfloat16
I32 = mybir.dt.int32
U32 = mybir.dt.uint32
U16 = mybir.dt.uint16
U8 = mybir.dt.uint8
FP8X4 = mybir.dt.float8_e4m3fn_x4
FP4X4 = mybir.dt.float4_e2m1fn_x4
ALU = mybir.AluOpType
ACT = mybir.ActivationFunctionType

P = 128
PACK = 4
T, S, H, G = 1024, 512, 512, 2048
LIST_COLS = S // 16
WIN = 2 * S
FLOPS = 4 * 2 * 512 * 512 * 512


def tile_picked_dthzaesndsndtwin_none_p_kernel(
    tc, x_words, x_scales, w1_words, w1_scales, w2_words, w2_scales, sl, th, gs, d_words, d_scales,
    offs, hz, n1, n2, ka, kb, n3, n4, out,
):
    nc = tc.nc
    with ExitStack() as ctx:
        lists = ctx.enter_context(tc.tile_pool(name="lists", bufs=1))
        keep = ctx.enter_context(tc.tile_pool(name="keep", bufs=1))
        psum = ctx.enter_context(tc.psum_pool(name="psum", bufs=1))

        def load_list(src, name):
            tile = lists.tile([P, LIST_COLS], U16, name=name)
            nc.sync.dma_start(tile[:], src)
            return tile

        def zeroed_bytes(width, name, tag=""):
            tile = keep.tile([P, width], U8, name=name, tag=tag, align_bytes=64)
            nc.vector.memset(tile[:].bitcast(I32), 0)
            return tile

        def to_plane(queue, plane, rows):
            for r in range(4):
                queue.dma_start(plane[r:P:32, :].bitcast(I32), rows[8 * r:P:32, :].bitcast(I32))

        x_bytes = zeroed_bytes(T, "x_bytes", tag="x_bytes")
        w_rows = zeroed_bytes(2 * H, "w_rows", tag="w_rows")
        d_bytes = zeroed_bytes(G, "d_bytes", tag="ds0")
        x_plane = zeroed_bytes(2 * S, "x_plane")
        d_plane = zeroed_bytes(2 * H, "d_plane")

        def load_words(src, name):
            raw = keep.tile([P, 2 * H], U8, name=name, tag=name, align_bytes=64)
            nc.sync.dma_start(raw[:].bitcast(I32), src[0].bitcast(I32))
            return raw

        def load_w_rows(queue, i, r):
            w_scales = (w1_scales, w2_scales)[i]
            queue.dma_start(w_rows[r:P:32, i * H:(i + 1) * H].bitcast(I32), w_scales[0, r:16:4, :].bitcast(I32))

        nc.scalar.dma_start(x_bytes[0:P:8, :].bitcast(I32), x_scales[0].bitcast(I32))
        hz_l = load_list(hz, "hz_l")
        offs_l = load_list(offs, "offs_l")
        ka_l = load_list(ka, "ka_l")
        kb_l = load_list(kb, "kb_l")
        load_w_rows(nc.sync, 0, 0)
        x_tab = keep.tile([P, T], I32, name="x_tab", tag="x_tab", align_bytes=64)
        nc.sync.dma_start(x_tab[:], x_words[0].rearrange("p n t -> p (n t)").bitcast(I32))
        w_raw = [load_words(w1_words, "w_raw0")]
        for i, r in ((0, 1), (0, 2), (0, 3), (1, 0), (1, 1)):
            load_w_rows(nc.sync, i, r)
        n1_l = load_list(n1, "n1_l")
        w_raw.append(load_words(w2_words, "w_raw1"))
        for r in (2, 3):
            load_w_rows(nc.gpsimd, 1, r)
        nc.gpsimd.dma_start(d_bytes[0:P:8, :].bitcast(I32), d_scales[0].bitcast(I32))

        xg_bytes = keep.tile([P, 2 * S], U8, name="xg_bytes", align_bytes=64)
        nc.vector.tensor_copy(xg_bytes[:, S:2 * S], x_bytes[:].indirect(hz_l[:]))
        nc.vector.tensor_copy(xg_bytes[:, 0:S], x_bytes[:].indirect(offs_l[:]))
        to_plane(nc.sync, x_plane, xg_bytes)

        n2_l = load_list(n2, "n2_l")
        n3_l = load_list(n3, "n3_l")
        n4_l = load_list(n4, "n4_l")
        xg_words = keep.tile([P, 2 * S], U32, name="xg_words", align_bytes=64)
        nc.vector.tensor_copy(xg_words[:, 0:S], x_tab[:].bitcast(U32).indirect(offs_l[:]))
        nc.vector.tensor_copy(xg_words[:, S:2 * S], x_tab[:].bitcast(U32).indirect(hz_l[:]))
        d_tab = keep.tile([P, G], I32, name="d_tab", tag="x_tab", align_bytes=64)
        nc.sync.dma_start(d_tab[:], d_words[0].rearrange("p n t -> p (n t)").bitcast(I32))

        w_plane = keep.tile([P, 2 * H], U8, name="w_plane", align_bytes=64)
        nc.vector.tensor_copy(
            w_plane[:].rearrange("p (w t m) -> p w t m", w=2, t=PACK),
            w_rows[:].rearrange("p (w m t) -> p w t m", w=2, t=PACK),
        )
        w_codes = []
        for i in range(2):
            codes = keep.tile([P, 2 * H], U8, name="w_codes%d" % i, align_bytes=64)
            nc.scalar.copy(
                codes[:].bitcast(U16).rearrange("p (t m) -> p t m", t=PACK),
                w_raw[i][:].bitcast(U16).rearrange("p (m t) -> p t m", t=PACK),
            )
            w_codes.append(codes)

        row_vals = []
        for name, src, tag in (("sl_t", sl, "w_raw0"), ("th_t", th, "w_raw1"), ("gs_t", gs, "x_bytes")):
            tile = keep.tile([P, PACK], F32, name=name, tag=tag, align_bytes=64)
            nc.gpsimd.dma_start(tile[:], src.rearrange("(p t) o -> p (t o)", t=PACK))
            row_vals.append(tile)
        sl_t, th_t, gs_t = row_vals

        dg_bytes = keep.tile([P, 2 * H], U8, name="dg_bytes", tag="w_rows", align_bytes=64)
        nc.vector.tensor_copy(dg_bytes[:, 0:H], d_bytes[:].indirect(ka_l[:]))
        nc.vector.tensor_copy(dg_bytes[:, H:2 * H], d_bytes[:].indirect(kb_l[:]))
        sl_th = keep.tile([P, PACK], F32, name="sl_th")
        nc.gpsimd.tensor_tensor(sl_th[:], sl_t[:], th_t[:], ALU.mult)
        neg_bias = keep.tile([P, PACK], F32, name="neg_bias", tag="z_quads", align_bytes=64)
        nc.gpsimd.tensor_scalar(neg_bias[:], sl_th[:], -1.0, 0.0, ALU.mult, ALU.add)
        dd_bytes = keep.tile([P, 2 * H], U8, name="dd_bytes", align_bytes=64)

        def deal_d_bytes(i):
            nc.vector.tensor_copy(
                dd_bytes[:, i * H:(i + 1) * H].rearrange("p (t m) -> p t m", t=PACK),
                dg_bytes[:, i * H:(i + 1) * H].rearrange("p (m t) -> p t m", t=PACK),
            )

        deal_d_bytes(0)

        y = []
        for t in range(PACK):
            acc = psum.tile([P, S], F32, name="y_acc%d" % t, tag="bank%d" % t)
            for i in range(2):
                nc.tensor.matmul_mx(
                    out=acc[:],
                    lhsT=w_codes[i][:, 2 * P * t:2 * P * (t + 1)].bitcast(FP4X4),
                    lhsT_scale=w_plane[:, i * H + P * t:i * H + P * (t + 1)],
                    rhs=xg_words[:, i * S:(i + 1) * S].bitcast(FP8X4),
                    rhs_scale=x_plane[:, i * S:(i + 1) * S],
                    start=(i == 0),
                    stop=(i == 1),
                )
            y_t = keep.tile([P, S], F32, name="y%d" % t, tag="y%d" % t, align_bytes=64)
            nc.scalar.copy(y_t[:], acc[:])
            y.append(y_t)

        z_quads = keep.tile([P, S, PACK], BF16, name="z_quads", tag="z_quads", align_bytes=64)
        ds, sg = [], []

        def send_y(t):
            ds_t = keep.tile([P, WIN], F32, name="ds%d" % t, tag="ds%d" % t, align_bytes=64)
            nc.vector.tensor_copy(ds_t[:].indirect(n1_l[:]), y[t][:])
            ds.append(ds_t)
            sg_t = keep.tile([P, S], F32, name="sg%d" % t)
            for half in range(2):
                nc.scalar.activation(
                    out=sg_t[:, half * S // 2:(half + 1) * S // 2],
                    in_=y[t][:].indirect(n2_l[:, half * LIST_COLS // 2:(half + 1) * LIST_COLS // 2]),
                    func=ACT.Sigmoid,
                    scale=sl_t[:, t:t + 1],
                    bias=neg_bias[:, t:t + 1],
                )
            sg.append(sg_t)

        def make_z(t, cols=slice(0, S)):
            gated = keep.tile([P, cols.stop - cols.start], F32, name="gated%d_%d" % (t, cols.start))
            nc.gpsimd.tensor_tensor(gated[:], ds[t][:, cols], sg[t][:, cols], ALU.mult)
            nc.scalar.activation(out=z_quads[:, cols, t], in_=gated[:], func=ACT.Copy, scale=gs_t[:, t:t + 1])

        dg_words = keep.tile([P, 2 * H], U32, name="dg_words", tag="y2", align_bytes=64)
        d_codes = [keep.tile([P, 2, 2, P], U32, name="d_codes%d" % u, align_bytes=64) for u in range(2)]

        send_y(0)
        deal_d_bytes(1)
        to_plane(nc.sync, d_plane, dd_bytes)
        send_y(1)
        make_z(0)
        send_y(2)
        make_z(1)
        send_y(3)
        make_z(2)
        head, middle, last, rest = slice(0, 128), slice(128, 384), slice(384, S), slice(128, S)
        z_codes = keep.tile([P, S], U32, name="z_codes", align_bytes=64)
        z_plane = keep.tile([P, S], U8, name="z_plane", align_bytes=64)

        def quantise(cols):
            nc.vector.quantize_mx(
                out=z_codes[:, cols].bitcast(FP8X4),
                scales=z_plane[:, cols],
                in_=z_quads[:, cols, :].rearrange("p c t -> p (c t)"),
            )

        def deal_d_words(u):
            nc.vector.tensor_copy(
                d_codes[u][:].rearrange("p w t (i m) -> p w i t m", m=4),
                dg_words[:].rearrange("p (w i m t) -> p w i t m", w=2, t=PACK, m=4)[:, :, :, 2 * u:2 * u + 2, :],
            )

        for cols in (slice(0, S // 2), slice(S // 2, S)):
            make_z(3, cols)
        nc.vector.tensor_copy(dg_words[:, 0:H], d_tab[:].bitcast(U32).indirect(ka_l[:]))
        nc.vector.tensor_copy(dg_words[:, H:2 * H], d_tab[:].bitcast(U32).indirect(kb_l[:]))
        quantise(head)
        deal_d_words(0)
        quantise(rest)
        deal_d_words(1)

        h2 = [keep.tile([P, 2, S], F32, name="h2_%d" % u) for u in range(2)]

        def second_product(bank, tiles, cols):
            width = cols.stop - cols.start
            acc = psum.tile([P, len(tiles), width], F32, name="h_acc%d" % bank, tag="bank%d" % bank)
            for j, t in enumerate(tiles):
                for i in range(2):
                    nc.tensor.matmul_mx(
                        out=acc[:, j, :],
                        lhsT=d_codes[t // 2][:, i, t % 2, :].bitcast(FP8X4),
                        lhsT_scale=d_plane[:, i * H + P * t:i * H + P * (t + 1)],
                        rhs=z_codes[:, cols].bitcast(FP8X4),
                        rhs_scale=z_plane[:, cols],
                        start=(i == 0),
                        stop=(i == 1),
                    )
            first = tiles[0]
            nc.scalar.activation(
                out=h2[first // 2][:, first % 2:first % 2 + len(tiles), cols], in_=acc[:], func=ACT.Copy, scale=0.0625
            )

        second_product(0, (0,), head)
        second_product(1, (1,), head)
        second_product(2, (0, 1), middle)
        second_product(3, (0, 1), last)
        second_product(4, (2, 3), slice(0, S // 2))
        second_product(5, (2, 3), slice(S // 2, S))

        ds2, st, ds3 = [], [], []
        out_rows = out.rearrange("(p t) s -> p t s", t=PACK)

        for t in range(PACK):
            ds2.append(keep.tile([P, WIN], F32, name="ds2_%d" % t))

        def send_h(t, cols):
            nc.vector.tensor_copy(
                ds2[t][:].indirect(n3_l[:, cols.start // 16:cols.stop // 16]), h2[t // 2][:, t % 2, cols]
            )

        def larger(t):
            st_t = keep.tile([P, S], F32, name="st%d" % t)
            nc.vector.tensor_tensor(st_t[:], h2[t // 2][:, t % 2, :], ds2[t][:, 0:S], ALU.max)
            st.append(st_t)

        def send_st(t):
            win = keep.tile([P, WIN], F32, name="ds3_%d" % t)
            nc.vector.tensor_copy(win[:].indirect(n4_l[:]), st[t][:])
            ds3.append(win)

        def finish(t):
            res = keep.tile([P, S], F32, name="res%d" % t)
            if t < PACK - 1:
                nc.gpsimd.tensor_tensor(res[:], st[t][:], ds3[t][:, 0:S], ALU.subtract)
                nc.sync.dma_start(out_rows[:, t, :], res[:])
            else:
                for queue, cols in ((nc.sync, slice(0, S // 2)), (nc.scalar, slice(S // 2, S))):
                    nc.vector.tensor_tensor(res[:, cols], st[t][:, cols], ds3[t][:, cols], ALU.subtract)
                    queue.dma_start(out_rows[:, t, cols], res[:, cols])

        for cols in (head, rest):
            send_h(0, cols)
            send_h(1, cols)
        larger(0)
        send_h(2, slice(0, S))
        larger(1)
        send_h(3, slice(0, S))
        larger(2)
        larger(3)
        send_st(0)
        for t in range(1, PACK):
            send_st(t)
            finish(t - 1)
        finish(PACK - 1)
